import numpy as np
import ml_dtypes


def mxq(x, axis, fmt="e4m3"):
    dtype, down = {"e4m3": (ml_dtypes.float8_e4m3fn, 7), "e5m2": (ml_dtypes.float8_e5m2, 14)}[fmt]
    v = np.moveaxis(np.asarray(x, np.float32).astype(ml_dtypes.bfloat16).astype(np.float64), axis, -1)
    blocks = v.reshape(v.shape[:-1] + (-1, 32))
    amax = np.abs(blocks).max(-1, keepdims=True)
    byte = np.maximum(np.where(amax > 0, np.frexp(amax)[1] - 1 + 127, 0) - down, 1)
    scale = np.exp2(byte - 127.0)
    codes = (blocks / scale).astype(np.float32).astype(dtype).astype(np.float64)
    return np.moveaxis((codes * scale).reshape(v.shape), -1, axis)


WIDE = False


def mx_kscale(k):
    if not WIDE:
        return np.ones(k)
    levels = np.array([10, -10, 5, -5, 0])
    if k % 512:
        return np.exp2(np.random.permutation(np.resize(levels, k // 32))).repeat(32)
    a = np.empty((k // 512, 16))
    for p in range(k // 512):
        a[p, :8] = np.random.permutation(np.resize(levels, 8))
        for g in range(8):
            far = levels[np.abs(levels - a[p, g]) >= 10]
            a[p, g + 8] = far[np.random.randint(len(far))]
    return np.exp2(a.ravel()).repeat(32)


def f64(x):
    return np.asarray(x).astype(np.float64)


def striped(idx):
    return np.tile(np.asarray(idx).reshape(-1, 16).T, (8, 1)).astype(np.uint16)


def unstriped(offs):
    return offs[:16].T.reshape(-1).astype(np.int64)


E2M1 = np.array([0.0, 0.5, 1.0, 1.5, 2.0, 3.0, 4.0, 6.0, -0.0, -0.5, -1.0, -1.5, -2.0, -3.0, -4.0, -6.0])


def pack_weight(w, fmt):
    k, n = w.shape
    w = f64(np.asarray(w, np.float32).astype(ml_dtypes.bfloat16)).reshape(k // 32, 32, n)
    amax = np.abs(w).max(1)
    if fmt == "e4m3":
        byte = np.frexp(amax)[1] - 1 + 127 - 7
    else:
        mant, ex = np.frexp(amax / 6.0)
        byte = np.where(mant > 0.5, ex, ex - 1) + 127
    byte = np.clip(np.where(amax > 0, byte, 1), 1, 254)
    scaled = (w * np.exp2(127.0 - byte)[:, None, :]).reshape(k, n).astype(np.float32)
    by_word = np.ascontiguousarray(scaled.reshape(k // 512, 128, 4, n).transpose(0, 1, 3, 2))
    if fmt == "e4m3":
        words = by_word.astype(ml_dtypes.float8_e4m3fn).view(np.uint8)
    else:
        c = by_word.astype(ml_dtypes.float4_e2m1fn).view(np.uint8) & 0xF
        words = (c[..., 0::2] | (c[..., 1::2] << 4)).reshape(k // 512, 128, 2 * n)
    return np.ascontiguousarray(words), np.ascontiguousarray(byte.astype(np.uint8).reshape(k // 512, 16, n))


def unpack_weight(words, scales, fmt):
    g, _, n = scales.shape
    words = np.ascontiguousarray(words).reshape(g, 128, n, -1)
    if fmt == "e4m3":
        vals = words.view(ml_dtypes.float8_e4m3fn).astype(np.float64)
    else:
        nib = np.empty((g, 128, n, 4), np.uint8)
        nib[..., 0::2] = words & 0xF
        nib[..., 1::2] = words >> 4
        vals = E2M1[nib]
    vals = vals * np.repeat(np.exp2(scales.astype(np.float64) - 127.0), 8, axis=1)[..., None]
    return vals.transpose(0, 1, 3, 2).reshape(g * 512, n)


def bf(x):
    return np.asarray(x, np.float32).astype(ml_dtypes.bfloat16)


def planes(Y):
    r, m = Y.shape
    b = f64(bf(Y)).reshape(r // 32, 32, m)
    amax = np.abs(b).max(1)
    byte = np.clip(np.where(amax > 0, np.frexp(amax)[1] - 1 + 127 - 7, 1), 1, 254)
    codes = (b * np.exp2(127.0 - byte)[:, None, :]).reshape(r, m).astype(np.float32).astype(ml_dtypes.float8_e4m3fn).view(np.uint8)
    words = codes.reshape(r // 512, 128, 4, m).transpose(0, 1, 3, 2)
    return np.ascontiguousarray(words), np.ascontiguousarray(byte.astype(np.uint8).reshape(r // 512, 16, m))


K, T, J, N = 1024, 1024, 512, 512


def setup_inputs():
    n = np.random.standard_normal
    idx = np.random.permutation(T)[:J]
    fk = mx_kscale(K)
    wap = pack_weight(n((K, N)) * 1 / np.sqrt(K) * fk[:, None], "e2m1")
    wbp = pack_weight(n((K, N)) * 1 / np.sqrt(K) * fk[:, None], "e4m3")
    wcp = pack_weight(n((K, N)) * 1 / np.sqrt(K) * fk[:, None], "e2m1")
    return {
        "xt": (n((K, T)) / fk[:, None]).astype(np.float32),
        "wa_words": wap[0],
        "wa_scales": wap[1],
        "wb_words": wbp[0],
        "wb_scales": wbp[1],
        "wc_words": wcp[0],
        "wc_scales": wcp[1],
        "ga": (np.random.uniform(0.4, 1.2, (1, J))).astype(np.float32),
        "res": (1.0 * n((N, T))).astype(np.float32),
        "offs": striped(idx),
    }


def reference(xt, wa_words, wa_scales, wb_words, wb_scales, wc_words, wc_scales, ga, res, offs):
    idx = unstriped(offs)
    wau = unpack_weight(wa_words, wa_scales, "e2m1")
    wbu = unpack_weight(wb_words, wb_scales, "e4m3")
    wcu = unpack_weight(wc_words, wc_scales, "e2m1")
    xtidxq = mxq(f64(xt)[:, idx], 0, "e4m3")
    a = wau.T @ xtidxq
    b = wbu.T @ xtidxq
    e = wcu.T @ xtidxq
    lo = np.minimum(a, b)
    hi = np.maximum(a, b)
    d = np.maximum(lo, np.minimum(hi, e)) * f64(ga)
    dp = np.zeros((N, T))
    dp[:, idx] = d
    y = 0.5 * f64(res) + dp
    words, scales = planes(y)
    return y, words, scales

@@ -1,0 +1,298 @@
+from contextlib import ExitStack
+
+import concourse.mybir as mybir
+from concourse.masks import make_identity
+
+K, T, J, N = 1024, 1024, 512, 512
+FLOPS = 3 * 2 * K * N * J
+
+F32 = mybir.dt.float32
+BF16 = mybir.dt.bfloat16
+I32 = mybir.dt.int32
+U32 = mybir.dt.uint32
+U16 = mybir.dt.uint16
+U8 = mybir.dt.uint8
+FP8X4 = mybir.dt.float8_e4m3fn_x4
+FP4X4 = mybir.dt.float4_e2m1fn_x4
+ALU = mybir.AluOpType
+COPY = mybir.ActivationFunctionType.Copy
+
+P = 128
+PACK = 4
+PASSES = K // (P * PACK)
+GROUPS = J // P
+LIST_COLS = P // 16
+QUARTERS = 4
+QCOLS = T // QUARTERS
+
+
+def tile_moe_middle_expert_of_three_pl_kernel(
+    tc, xt, wa_words, wa_scales, wb_words, wb_scales, wc_words, wc_scales, ga, res, offs, out_0, out_1, out_2
+):
+    nc = tc.nc
+    with ExitStack() as ctx:
+        keep = ctx.enter_context(tc.tile_pool(name="keep", bufs=1))
+        ring = ctx.enter_context(tc.tile_pool(name="ring", bufs=2))
+        psum = ctx.enter_context(tc.psum_pool(name="psum", bufs=2))
+
+        offsets = keep.tile([P, J // 16], U16, name="offsets")
+        nc.sync.dma_start(offsets[:], offs)
+
+        experts = (
+            (wa_words, wa_scales, FP4X4, 2),
+            (wb_words.rearrange("z p c r -> z p (c r)"), wb_scales, FP8X4, 4),
+            (wc_words, wc_scales, FP4X4, 2),
+        )
+        w_scales = []
+        for e in range(3):
+            plane = keep.tile([P, PASSES * N], U8, name="w_scales%d" % e, align_bytes=64)
+            nc.gpsimd.memset(plane[:].bitcast(I32), 0)
+            w_scales.append(plane)
+
+        x_rows = xt.rearrange("(z p t) c -> z t p c", z=PASSES, t=PACK)
+        x_planes = {}
+        w_words = {}
+
+        def load_x(z, t):
+            x_planes[z, t] = keep.tile([P, T], F32, name="x%d%d" % (z, t))
+            nc.sync.dma_start(x_planes[z, t][:], x_rows[z, t])
+
+        def load_words(e, z):
+            words, scales, dtype, width = experts[e]
+            w_words[e, z] = keep.tile([P, width * N], U8, name="w_words%d%d" % (e, z), align_bytes=64)
+            nc.sync.dma_start(w_words[e, z][:].bitcast(I32), words[z].bitcast(I32))
+
+        def load_scales(e, first_row):
+            rows = experts[e][1].bitcast(I32).rearrange("z (q r) c -> r q z c", r=4)
+            for r in (first_row, first_row + 1):
+                nc.sync.dma_start(
+                    w_scales[e][r:P:32, :].bitcast(I32).rearrange("q (z c) -> q z c", z=PASSES), rows[r]
+                )
+
+        load_x(0, 0)
+        load_x(0, 1)
+        load_scales(0, 0)
+        load_x(0, 2)
+        load_scales(0, 2)
+        load_x(0, 3)
+        load_scales(1, 0)
+        load_words(0, 0)
+        load_words(1, 0)
+        load_scales(1, 2)
+        load_x(1, 0)
+        load_scales(2, 0)
+        load_x(1, 1)
+        load_scales(2, 2)
+        load_words(2, 0)
+        load_x(1, 2)
+        load_x(1, 3)
+        for e in range(3):
+            load_words(e, 1)
+        res_rows = res.rearrange("(p t) c -> t p c", t=PACK)
+        res_planes = []
+        for t in range(PACK):
+            plane = keep.tile([P, T], F32, name="res%d" % t)
+            nc.sync.dma_start(plane[:], res_rows[t])
+            res_planes.append(plane)
+
+        identity = keep.tile([P, P], F32, name="identity")
+        make_identity(nc, identity[:])
+        ga_rows = keep.tile([P, P], F32, name="ga_rows")
+        nc.gpsimd.memset(ga_rows[:], 0.0)
+        nc.scalar.dma_start(ga_rows[0:GROUPS, :], ga.rearrange("o (g p) -> (o g) p", p=P))
+        turned = psum.tile([P, PACK, P], F32, name="turned")
+        nc.tensor.transpose(turned[:, 0, :], ga_rows[:], identity[:])
+        gate = keep.tile([P, GROUPS], F32, name="gate")
+        nc.scalar.activation(gate[:], turned[:, 0, 0:GROUPS], COPY)
+
+        x_codes = {}
+        x_scales = {}
+        picked = {}
+        for z, lo, hi in ((0, 0, GROUPS), (1, 0, 1), (1, 1, GROUPS)):
+            picked[z, lo, hi] = keep.tile([P, PACK, (hi - lo) * P], F32, name="picked%d%d" % (z, lo))
+
+        def gather(z, t, lo, hi):
+            nc.vector.tensor_copy(
+                picked[z, lo, hi][:, t, :],
+                x_planes[z, t][:].indirect(offsets[:, lo * LIST_COLS : hi * LIST_COLS]),
+            )
+
+        def weave(z, g, count, lo, hi):
+            woven = keep.tile([P, count * P, PACK], BF16, name="woven%d%d" % (z, g), align_bytes=64)
+            nc.scalar.copy(
+                woven[:].rearrange("p (c i) t -> p c t i", i=4),
+                picked[z, lo, hi][:, :, (g - lo) * P : (g - lo + count) * P].rearrange("p t (c i) -> p c t i", i=4),
+            )
+            return woven
+
+        def quantise(z, g, count, woven):
+            codes = keep.tile([P, count * P], U32, name="x_codes%d%d" % (z, g), align_bytes=64)
+            scales = keep.tile([P, count * P], U8, name="x_scales%d%d" % (z, g), align_bytes=64)
+            nc.vector.quantize_mx(
+                out=codes[:].bitcast(FP8X4),
+                scales=scales[:],
+                in_=woven[:].rearrange("p c t -> p (c t)"),
+            )
+            for n in range(count):
+                x_codes[z, g + n] = codes[:, n * P : (n + 1) * P]
+                x_scales[z, g + n] = scales[:, n * P : (n + 1) * P]
+
+        sums = {}
+
+        def multiply(e, z, g):
+            if z == 0:
+                sums[e, g] = psum.tile([P, N], F32, name="sum%d" % e)
+            nc.tensor.matmul_mx(
+                out=sums[e, g][:],
+                lhsT=x_codes[z, g].bitcast(FP8X4),
+                lhsT_scale=x_scales[z, g],
+                rhs=w_words[e, z][:].bitcast(experts[e][2]),
+                rhs_scale=w_scales[e][:, z * N : (z + 1) * N],
+                start=(z == 0),
+                stop=(z == PASSES - 1),
+            )
+
+        for t in range(PACK):
+            gather(0, t, 0, GROUPS)
+        first = [weave(0, g, 2, 0, GROUPS) for g in (0, 2)]
+        for t in range(PACK):
+            gather(1, t, 0, 1)
+            gather(1, t, 1, GROUPS)
+            if t == 0:
+                quantise(0, 0, 2, first[0])
+                quantise(0, 2, 2, first[1])
+                for g in range(2):
+                    for e in range(3):
+                        multiply(e, 0, g)
+        quantise(1, 0, 1, weave(1, 0, 1, 0, 1))
+        quantise(1, 1, 1, weave(1, 1, 1, 1, GROUPS))
+        quantise(1, 2, 2, weave(1, 2, 2, 1, GROUPS))
+
+        windows = []
+        for t in range(PACK):
+            window = keep.tile([P, T], F32, name="window%d" % t)
+            (nc.vector if t < 2 else nc.gpsimd).memset(window[:], 0.0)
+            windows.append(window)
+
+        def dealt(bank):
+            return bank[:].rearrange("p (m t) -> p t m", t=PACK)
+
+        placed = keep.tile([P, PACK, J], F32, name="placed")
+        held = {}
+
+        def upper(g):
+            for e in range(3):
+                if g >= 2:
+                    multiply(e, 0, g)
+                multiply(e, 1, g)
+            first_answer = ring.tile([P, PACK, P], F32, name="first_answer", tag="scalar_made")
+            if g == 0:
+                nc.vector.tensor_scalar(first_answer[:], dealt(sums[0, g]), gate[:, g : g + 1], None, ALU.mult)
+            else:
+                nc.scalar.activation(first_answer[:], dealt(sums[0, g]), COPY, scale=gate[:, g : g + 1])
+            hi = ring.tile([P, PACK, P], F32, name="hi")
+            nc.vector.scalar_tensor_tensor(
+                hi[:], dealt(sums[1, g]), gate[:, g : g + 1], first_answer[:], ALU.mult, ALU.max
+            )
+            held[g] = (first_answer, hi)
+
+        def lower(g):
+            first_answer, hi = held[g]
+            lo = ring.tile([P, PACK, P], F32, name="lo")
+            nc.vector.scalar_tensor_tensor(
+                lo[:], dealt(sums[1, g]), gate[:, g : g + 1], first_answer[:], ALU.mult, ALU.min
+            )
+            capped = ring.tile([P, PACK, P], F32, name="capped")
+            nc.vector.scalar_tensor_tensor(
+                capped[:], dealt(sums[2, g]), gate[:, g : g + 1], hi[:], ALU.mult, ALU.min
+            )
+            held[g] = (lo, capped)
+
+        def middle(g):
+            lo, capped = held[g]
+            mid = ring.tile([P, PACK, P], F32, name="mid")
+            nc.vector.tensor_tensor(mid[:], lo[:], capped[:], ALU.max)
+            turned = psum.tile([P, PACK, P], F32, name="turned")
+            for t in range(PACK):
+                nc.tensor.transpose(turned[:, t, :], mid[:, t, :], identity[:])
+            nc.scalar.copy(placed[:, :, g * P : (g + 1) * P], turned[:])
+
+        upper(0)
+        lower(0)
+        for g in range(1, GROUPS):
+            upper(g)
+            middle(g - 1)
+            lower(g)
+        middle(GROUPS - 1)
+
+        def scatter(t, lo, hi):
+            nc.vector.tensor_copy(
+                windows[t][:].indirect(offsets[:, lo * LIST_COLS : hi * LIST_COLS]),
+                placed[:, t, lo * P : hi * P],
+            )
+
+        out_rows = out_0.rearrange("(p t) c -> t p c", t=PACK)
+        y_early = keep.tile([P, 2, T], F32, name="y_early")
+        y_woven = [keep.tile([P, QCOLS, PACK], BF16, name="y_woven%d" % q, align_bytes=64) for q in range(QUARTERS)]
+        quarters = [slice(q * QCOLS, (q + 1) * QCOLS) for q in range(QUARTERS)]
+
+        def weave_pair(u, q, source, copy):
+            copy(
+                y_woven[q][:, :, 2 * u : 2 * u + 2].rearrange("p (c i) t -> p c t i", i=4),
+                source.rearrange("p t (c i) -> p c t i", i=4),
+            )
+
+        def halve(t):
+            halved = ring.tile([P, T], F32, name="halved", tag="scalar_made")
+            nc.scalar.activation(halved[:], res_planes[t][:], COPY, scale=0.5)
+            return halved
+
+        scatter(0, 0, 2)
+        scatter(1, 0, 2)
+        for t in range(2):
+            scatter(t, 2, GROUPS)
+            nc.gpsimd.tensor_tensor(y_early[:, t, :], windows[t][:], halve(t)[:], ALU.add)
+            nc.sync.dma_start(out_rows[t], y_early[:, t, :])
+        scatter(2, 0, GROUPS)
+        y_late = ring.tile([P, 2 * T], F32, name="y_late", tag="scalar_made")
+        by_plane = y_late[:].rearrange("p (q t c) -> p t q c", q=QUARTERS, t=2)
+
+        def late(q, t):
+            return y_late[:, (2 * q + t) * QCOLS : (2 * q + t + 1) * QCOLS]
+
+        def quartered(plane):
+            return plane[:].rearrange("p (q c) -> p q c", q=QUARTERS)
+
+        nc.scalar.activation(by_plane[:, 1], quartered(res_planes[2]), COPY, scale=0.5)
+        for q in range(QUARTERS):
+            weave_pair(0, q, y_early[:, :, quarters[q]], nc.scalar.copy)
+        nc.gpsimd.tensor_tensor(by_plane[:, 0], quartered(windows[2]), by_plane[:, 1], ALU.add)
+        for q in range(QUARTERS):
+            nc.sync.dma_start(out_rows[2][:, quarters[q]], late(q, 0))
+        last = PACK - 1
+        scatter(last, 0, GROUPS)
+        for q in range(QUARTERS):
+            nc.vector.scalar_tensor_tensor(
+                late(q, 1), res_planes[last][:, quarters[q]], 0.5, windows[last][:, quarters[q]], ALU.mult, ALU.add
+            )
+            nc.sync.dma_start(out_rows[last][:, quarters[q]], late(q, 1))
+        for q in range(QUARTERS):
+            pair = y_late[:, 2 * q * QCOLS : 2 * (q + 1) * QCOLS].rearrange("p (t c) -> p t c", t=2)
+            weave_pair(1, q, pair, nc.scalar.copy if q < QUARTERS - 1 else nc.vector.tensor_copy)
+
+        y_codes = keep.tile([P, T], U32, name="y_codes", align_bytes=64)
+        y_scales = keep.tile([P, T], U8, name="y_scales", align_bytes=64)
+        word_rows = out_1[0].rearrange("p c r -> p (c r)").bitcast(I32)
+        for q in (0, 3, 1, 2):
+            cols = slice(q * QCOLS, (q + 1) * QCOLS)
+            nc.vector.quantize_mx(
+                out=y_codes[:, cols].bitcast(FP8X4),
+                scales=y_scales[:, cols],
+                in_=y_woven[q][:].rearrange("p c t -> p (c t)"),
+            )
+            nc.sync.dma_start(word_rows[:, cols], y_codes[:, cols].bitcast(I32))
+        scale_rows = out_2[0].bitcast(I32)
+        for quad in range(4):
+            nc.scalar.dma_start(
+                scale_rows[4 * quad : 4 * quad + 4, :], y_scales[32 * quad : 32 * quad + 4, :].bitcast(I32)
+            )

@@ -36,7 +36,6 @@ def tile_moe_middle_expert_of_three_pl_kernel(
         psum = ctx.enter_context(tc.psum_pool(name="psum", bufs=2))
 
         offsets = keep.tile([P, J // 16], U16, name="offsets")
-        nc.sync.dma_start(offsets[:], offs)
 
         experts = (
             (wa_words, wa_scales, FP4X4, 2),
@@ -54,40 +53,44 @@ def tile_moe_middle_expert_of_three_pl_kernel(
         w_words = {}
 
         def load_x(z, t):
-            x_planes[z, t] = keep.tile([P, T], F32, name="x%d%d" % (z, t))
+            x_planes[z, t] = keep.tile([P, T], F32, name="x%d%d" % (z, t), align_bytes=64)
             nc.sync.dma_start(x_planes[z, t][:], x_rows[z, t])
 
-        def load_words(e, z):
+        def load_words(e, passes):
             words, scales, dtype, width = experts[e]
-            w_words[e, z] = keep.tile([P, width * N], U8, name="w_words%d%d" % (e, z), align_bytes=64)
-            nc.sync.dma_start(w_words[e, z][:].bitcast(I32), words[z].bitcast(I32))
+            tile = keep.tile([P, len(passes) * width * N], U8, name="w_words%d%d" % (e, passes[0]), align_bytes=64)
+            nc.sync.dma_start(
+                tile[:].bitcast(I32).rearrange("p (z c) -> p z c", z=len(passes)),
+                words[passes[0] : passes[-1] + 1].bitcast(I32).rearrange("z p c -> p z c"),
+            )
+            for n, z in enumerate(passes):
+                w_words[e, z] = tile[:, n * width * N : (n + 1) * width * N]
 
-        def load_scales(e, first_row):
+        def load_scales(e, r, queue):
             rows = experts[e][1].bitcast(I32).rearrange("z (q r) c -> r q z c", r=4)
-            for r in (first_row, first_row + 1):
-                nc.sync.dma_start(
-                    w_scales[e][r:P:32, :].bitcast(I32).rearrange("q (z c) -> q z c", z=PASSES), rows[r]
-                )
+            queue.dma_start(w_scales[e][r:P:32, :].bitcast(I32).rearrange("q (z c) -> q z c", z=PASSES), rows[r])
 
         load_x(0, 0)
+        nc.sync.dma_start(offsets[:], offs)
         load_x(0, 1)
-        load_scales(0, 0)
         load_x(0, 2)
-        load_scales(0, 2)
         load_x(0, 3)
-        load_scales(1, 0)
-        load_words(0, 0)
-        load_words(1, 0)
-        load_scales(1, 2)
+        load_scales(0, 0, nc.sync)
         load_x(1, 0)
-        load_scales(2, 0)
+        load_scales(0, 1, nc.sync)
+        load_words(1, [0])
+        load_words(0, [0, 1])
+        load_scales(0, 2, nc.sync)
         load_x(1, 1)
-        load_scales(2, 2)
-        load_words(2, 0)
+        load_scales(0, 3, nc.sync)
         load_x(1, 2)
         load_x(1, 3)
-        for e in range(3):
-            load_words(e, 1)
+        load_words(1, [1])
+        load_scales(2, 0, nc.sync)
+        load_scales(2, 1, nc.sync)
+        load_words(2, [0, 1])
+        load_scales(2, 2, nc.sync)
+        load_scales(2, 3, nc.sync)
         res_rows = res.rearrange("(p t) c -> t p c", t=PACK)
         res_planes = []
         for t in range(PACK):
@@ -99,7 +102,9 @@ def tile_moe_middle_expert_of_three_pl_kernel(
         make_identity(nc, identity[:])
         ga_rows = keep.tile([P, P], F32, name="ga_rows")
         nc.gpsimd.memset(ga_rows[:], 0.0)
-        nc.scalar.dma_start(ga_rows[0:GROUPS, :], ga.rearrange("o (g p) -> (o g) p", p=P))
+        nc.gpsimd.dma_start(ga_rows[0:GROUPS, :], ga.rearrange("o (g p) -> (o g) p", p=P))
+        for r in range(4):
+            load_scales(1, r, nc.gpsimd)
         turned = psum.tile([P, PACK, P], F32, name="turned")
         nc.tensor.transpose(turned[:, 0, :], ga_rows[:], identity[:])
         gate = keep.tile([P, GROUPS], F32, name="gate")
@@ -125,8 +130,8 @@ def tile_moe_middle_expert_of_three_pl_kernel(
             )
             return woven
 
-        def quantise(z, g, count, woven):
-            codes = keep.tile([P, count * P], U32, name="x_codes%d%d" % (z, g), align_bytes=64)
+        def quantise(z, g, count, woven, slot):
+            codes = keep.tile([P, count * P], U32, name="x_codes", tag=slot, align_bytes=64)
             scales = keep.tile([P, count * P], U8, name="x_scales%d%d" % (z, g), align_bytes=64)
             nc.vector.quantize_mx(
                 out=codes[:].bitcast(FP8X4),
@@ -146,7 +151,7 @@ def tile_moe_middle_expert_of_three_pl_kernel(
                 out=sums[e, g][:],
                 lhsT=x_codes[z, g].bitcast(FP8X4),
                 lhsT_scale=x_scales[z, g],
-                rhs=w_words[e, z][:].bitcast(experts[e][2]),
+                rhs=w_words[e, z].bitcast(experts[e][2]),
                 rhs_scale=w_scales[e][:, z * N : (z + 1) * N],
                 start=(z == 0),
                 stop=(z == PASSES - 1),
@@ -159,20 +164,20 @@ def tile_moe_middle_expert_of_three_pl_kernel(
             gather(1, t, 0, 1)
             gather(1, t, 1, GROUPS)
             if t == 0:
-                quantise(0, 0, 2, first[0])
-                quantise(0, 2, 2, first[1])
+                quantise(0, 0, 2, first[0], "x10")
                 for g in range(2):
-                    for e in range(3):
+                    for e in range(2):
                         multiply(e, 0, g)
-        quantise(1, 0, 1, weave(1, 0, 1, 0, 1))
-        quantise(1, 1, 1, weave(1, 1, 1, 1, GROUPS))
-        quantise(1, 2, 2, weave(1, 2, 2, 1, GROUPS))
+            if t == 1:
+                quantise(0, 2, 2, first[1], "x11")
+        quantise(1, 0, 1, weave(1, 0, 1, 0, 1), "codes10")
+        quantise(1, 1, 1, weave(1, 1, 1, 1, GROUPS), "codes11")
+        quantise(1, 2, 2, weave(1, 2, 2, 1, GROUPS), "codes12")
 
-        windows = []
-        for t in range(PACK):
-            window = keep.tile([P, T], F32, name="window%d" % t)
-            (nc.vector if t < 2 else nc.gpsimd).memset(window[:], 0.0)
-            windows.append(window)
+        windows = {}
+        for t, engine in ((0, nc.vector), (2, nc.vector), (3, nc.vector)):
+            windows[t] = keep.tile([P, T], F32, name="window%d" % t)
+            engine.memset(windows[t][:], 0.0)
 
         def dealt(bank):
             return bank[:].rearrange("p (m t) -> p t m", t=PACK)
@@ -182,15 +187,15 @@ def tile_moe_middle_expert_of_three_pl_kernel(
 
         def upper(g):
             for e in range(3):
-                if g >= 2:
+                if g >= 2 or e == 2:
                     multiply(e, 0, g)
                 multiply(e, 1, g)
-            first_answer = ring.tile([P, PACK, P], F32, name="first_answer", tag="scalar_made")
+            first_answer = keep.tile([P, PACK, P], F32, name="first_answer", tag="first%d" % g)
             if g == 0:
                 nc.vector.tensor_scalar(first_answer[:], dealt(sums[0, g]), gate[:, g : g + 1], None, ALU.mult)
             else:
                 nc.scalar.activation(first_answer[:], dealt(sums[0, g]), COPY, scale=gate[:, g : g + 1])
-            hi = ring.tile([P, PACK, P], F32, name="hi")
+            hi = keep.tile([P, PACK, P], F32, name="hi", tag="hi%d" % g)
             nc.vector.scalar_tensor_tensor(
                 hi[:], dealt(sums[1, g]), gate[:, g : g + 1], first_answer[:], ALU.mult, ALU.max
             )
@@ -210,7 +215,7 @@ def tile_moe_middle_expert_of_three_pl_kernel(
 
         def middle(g):
             lo, capped = held[g]
-            mid = ring.tile([P, PACK, P], F32, name="mid")
+            mid = keep.tile([P, PACK, P], F32, name="mid", tag="mid%d" % g)
             nc.vector.tensor_tensor(mid[:], lo[:], capped[:], ALU.max)
             turned = psum.tile([P, PACK, P], F32, name="turned")
             for t in range(PACK):
@@ -243,10 +248,12 @@ def tile_moe_middle_expert_of_three_pl_kernel(
             )
 
         def halve(t):
-            halved = ring.tile([P, T], F32, name="halved", tag="scalar_made")
+            halved = keep.tile([P, T], F32, name="halved", tag=("first2", "hi3")[t])
             nc.scalar.activation(halved[:], res_planes[t][:], COPY, scale=0.5)
             return halved
 
+        windows[1] = keep.tile([P, T], F32, name="window1", tag="first3")
+        nc.gpsimd.memset(windows[1][:], 0.0)
         scatter(0, 0, 2)
         scatter(1, 0, 2)
         for t in range(2):
@@ -254,7 +261,7 @@ def tile_moe_middle_expert_of_three_pl_kernel(
             nc.gpsimd.tensor_tensor(y_early[:, t, :], windows[t][:], halve(t)[:], ALU.add)
             nc.sync.dma_start(out_rows[t], y_early[:, t, :])
         scatter(2, 0, GROUPS)
-        y_late = ring.tile([P, 2 * T], F32, name="y_late", tag="scalar_made")
+        y_late = keep.tile([P, 2 * T], F32, name="y_late", tag="mid3")
         by_plane = y_late[:].rearrange("p (q t c) -> p t q c", q=QUARTERS, t=2)
 
         def late(q, t):
@@ -275,7 +282,7 @@ def tile_moe_middle_expert_of_three_pl_kernel(
             nc.vector.scalar_tensor_tensor(
                 late(q, 1), res_planes[last][:, quarters[q]], 0.5, windows[last][:, quarters[q]], ALU.mult, ALU.add
             )
-            nc.sync.dma_start(out_rows[last][:, quarters[q]], late(q, 1))
+        nc.sync.dma_start(out_rows[last].rearrange("p (q c) -> p q c", q=QUARTERS), by_plane[:, 1])
         for q in range(QUARTERS):
             pair = y_late[:, 2 * q * QCOLS : 2 * (q + 1) * QCOLS].rearrange("p (t c) -> p t c", t=2)
             weave_pair(1, q, pair, nc.scalar.copy if q < QUARTERS - 1 else nc.vector.tensor_copy)
@@ -290,7 +297,9 @@ def tile_moe_middle_expert_of_three_pl_kernel(
                 scales=y_scales[:, cols],
                 in_=y_woven[q][:].rearrange("p c t -> p (c t)"),
             )
-            nc.sync.dma_start(word_rows[:, cols], y_codes[:, cols].bitcast(I32))
+            if q != 1:
+                ready = slice(QCOLS, 3 * QCOLS) if q == 2 else cols
+                nc.sync.dma_start(word_rows[:, ready], y_codes[:, ready].bitcast(I32))
         scale_rows = out_2[0].bitcast(I32)
         for quad in range(4):
             nc.scalar.dma_start(

@@ -16,14 +16,15 @@ FP8X4 = mybir.dt.float8_e4m3fn_x4
 FP4X4 = mybir.dt.float4_e2m1fn_x4
 ALU = mybir.AluOpType
 COPY = mybir.ActivationFunctionType.Copy
+RELU = mybir.ActivationFunctionType.Relu
 
 P = 128
 PACK = 4
 PASSES = K // (P * PACK)
 GROUPS = J // P
 LIST_COLS = P // 16
-QUARTERS = 4
-QCOLS = T // QUARTERS
+QCOLS = T // 4
+VECTOR_FROM = 640
 
 
 def tile_moe_middle_expert_of_three_pl_kernel(
@@ -32,7 +33,6 @@ def tile_moe_middle_expert_of_three_pl_kernel(
     nc = tc.nc
     with ExitStack() as ctx:
         keep = ctx.enter_context(tc.tile_pool(name="keep", bufs=1))
-        ring = ctx.enter_context(tc.tile_pool(name="ring", bufs=2))
         psum = ctx.enter_context(tc.psum_pool(name="psum", bufs=2))
 
         offsets = keep.tile([P, J // 16], U16, name="offsets")
@@ -112,21 +112,21 @@ def tile_moe_middle_expert_of_three_pl_kernel(
 
         x_codes = {}
         x_scales = {}
-        picked = {}
-        for z, lo, hi in ((0, 0, GROUPS), (1, 0, 1), (1, 1, GROUPS)):
-            picked[z, lo, hi] = keep.tile([P, PACK, (hi - lo) * P], F32, name="picked%d%d" % (z, lo))
+        picked = [keep.tile([P, PACK * J], F32, name="picked%d" % z) for z in range(PASSES)]
 
         def gather(z, t, lo, hi):
             nc.vector.tensor_copy(
-                picked[z, lo, hi][:, t, :],
+                picked[z][:, t * J + lo * P : t * J + hi * P],
                 x_planes[z, t][:].indirect(offsets[:, lo * LIST_COLS : hi * LIST_COLS]),
             )
 
-        def weave(z, g, count, lo, hi):
+        def weave(z, g, count):
             woven = keep.tile([P, count * P, PACK], BF16, name="woven%d%d" % (z, g), align_bytes=64)
             nc.scalar.copy(
                 woven[:].rearrange("p (c i) t -> p c t i", i=4),
-                picked[z, lo, hi][:, :, (g - lo) * P : (g - lo + count) * P].rearrange("p t (c i) -> p c t i", i=4),
+                picked[z][:]
+                .rearrange("p (t j) -> p t j", t=PACK)[:, :, g * P : (g + count) * P]
+                .rearrange("p t (c i) -> p c t i", i=4),
             )
             return woven
 
@@ -159,23 +159,22 @@ def tile_moe_middle_expert_of_three_pl_kernel(
 
         for t in range(PACK):
             gather(0, t, 0, GROUPS)
-        first = [weave(0, g, 2, 0, GROUPS) for g in (0, 2)]
-        for t in range(PACK):
-            gather(1, t, 0, 1)
-            gather(1, t, 1, GROUPS)
-            if t == 0:
-                quantise(0, 0, 2, first[0], "x10")
-                for g in range(2):
-                    for e in range(2):
-                        multiply(e, 0, g)
-            if t == 1:
-                quantise(0, 2, 2, first[1], "x11")
-        quantise(1, 0, 1, weave(1, 0, 1, 0, 1), "codes10")
-        quantise(1, 1, 1, weave(1, 1, 1, 1, GROUPS), "codes11")
-        quantise(1, 2, 2, weave(1, 2, 2, 1, GROUPS), "codes12")
+        first = [weave(0, 0, 1), weave(0, 1, 1), weave(0, 2, 2)]
+        for t in range(PACK - 1):
+            gather(1, t, 0, GROUPS)
+            if t < 2:
+                quantise(0, t, 1, first[t], "x1%d" % t)
+                for e in range(2):
+                    multiply(e, 0, t)
+        gather(1, PACK - 1, 0, 1)
+        gather(1, PACK - 1, 1, GROUPS)
+        quantise(1, 0, 1, weave(1, 0, 1), "codes10")
+        quantise(0, 2, 2, first[2], "x13")
+        quantise(1, 1, 1, weave(1, 1, 1), "codes11")
+        quantise(1, 2, 2, weave(1, 2, 2), "codes12")
 
         windows = {}
-        for t, engine in ((0, nc.vector), (2, nc.vector), (3, nc.vector)):
+        for t, engine in ((0, nc.vector), (1, nc.vector), (2, nc.vector), (3, nc.gpsimd)):
             windows[t] = keep.tile([P, T], F32, name="window%d" % t)
             engine.memset(windows[t][:], 0.0)
 
@@ -183,52 +182,54 @@ def tile_moe_middle_expert_of_three_pl_kernel(
             return bank[:].rearrange("p (m t) -> p t m", t=PACK)
 
         placed = keep.tile([P, PACK, J], F32, name="placed")
-        held = {}
 
-        def upper(g):
+        def compare(g):
             for e in range(3):
                 if g >= 2 or e == 2:
                     multiply(e, 0, g)
                 multiply(e, 1, g)
-            first_answer = keep.tile([P, PACK, P], F32, name="first_answer", tag="first%d" % g)
+            weight = gate[:, g : g + 1]
+            first_answer = keep.tile([P, PACK, P], F32, name="first_answer%d" % g)
             if g == 0:
-                nc.vector.tensor_scalar(first_answer[:], dealt(sums[0, g]), gate[:, g : g + 1], None, ALU.mult)
+                nc.vector.tensor_scalar(first_answer[:], dealt(sums[0, g]), weight, None, ALU.mult)
             else:
-                nc.scalar.activation(first_answer[:], dealt(sums[0, g]), COPY, scale=gate[:, g : g + 1])
-            hi = keep.tile([P, PACK, P], F32, name="hi", tag="hi%d" % g)
-            nc.vector.scalar_tensor_tensor(
-                hi[:], dealt(sums[1, g]), gate[:, g : g + 1], first_answer[:], ALU.mult, ALU.max
-            )
-            held[g] = (first_answer, hi)
+                nc.scalar.activation(first_answer[:], dealt(sums[0, g]), COPY, scale=weight)
+            hi = keep.tile([P, PACK, P], F32, name="hi%d" % g)
+            nc.vector.scalar_tensor_tensor(hi[:], dealt(sums[1, g]), weight, first_answer[:], ALU.mult, ALU.max)
+            lo = keep.tile([P, PACK, P], F32, name="lo%d" % g)
+            nc.vector.scalar_tensor_tensor(lo[:], dealt(sums[1, g]), weight, first_answer[:], ALU.mult, ALU.min)
+            capped = keep.tile([P, PACK, P], F32, name="capped%d" % g)
+            nc.vector.scalar_tensor_tensor(capped[:], dealt(sums[2, g]), weight, hi[:], ALU.mult, ALU.min)
+            other = keep.tile([P, PACK, P], F32, name="other", tag="other%d" % g)
+            if g < GROUPS - 1:
+                nc.gpsimd.tensor_tensor(other[:], lo[:], capped[:], ALU.subtract)
+            else:
+                nc.vector.tensor_tensor(other[:], lo[:], capped[:], ALU.max)
+            return capped, other
 
-        def lower(g):
-            first_answer, hi = held[g]
-            lo = ring.tile([P, PACK, P], F32, name="lo")
-            nc.vector.scalar_tensor_tensor(
-                lo[:], dealt(sums[1, g]), gate[:, g : g + 1], first_answer[:], ALU.mult, ALU.min
-            )
-            capped = ring.tile([P, PACK, P], F32, name="capped")
-            nc.vector.scalar_tensor_tensor(
-                capped[:], dealt(sums[2, g]), gate[:, g : g + 1], hi[:], ALU.mult, ALU.min
-            )
-            held[g] = (lo, capped)
-
-        def middle(g):
-            lo, capped = held[g]
-            mid = keep.tile([P, PACK, P], F32, name="mid", tag="mid%d" % g)
-            nc.vector.tensor_tensor(mid[:], lo[:], capped[:], ALU.max)
+        def place(g, capped, other):
+            if g < GROUPS - 1:
+                lift = keep.tile([P, PACK, P], F32, name="lift%d" % g)
+                nc.scalar.activation(lift[:], other[:], RELU)
+                parts = (capped, lift)
+            else:
+                parts = (other,)
             turned = psum.tile([P, PACK, P], F32, name="turned")
             for t in range(PACK):
-                nc.tensor.transpose(turned[:, t, :], mid[:, t, :], identity[:])
+                for n, source in enumerate(parts):
+                    nc.tensor.matmul(
+                        turned[:, t, :],
+                        source[:, t, :],
+                        identity[:],
+                        start=n == 0,
+                        stop=n == len(parts) - 1,
+                        is_transpose=True,
+                    )
             nc.scalar.copy(placed[:, :, g * P : (g + 1) * P], turned[:])
 
-        upper(0)
-        lower(0)
-        for g in range(1, GROUPS):
-            upper(g)
-            middle(g - 1)
-            lower(g)
-        middle(GROUPS - 1)
+        compared = [compare(g) for g in range(GROUPS)]
+        for g in range(GROUPS):
+            place(g, *compared[g])
 
         def scatter(t, lo, hi):
             nc.vector.tensor_copy(
@@ -237,69 +238,58 @@ def tile_moe_middle_expert_of_three_pl_kernel(
             )
 
         out_rows = out_0.rearrange("(p t) c -> t p c", t=PACK)
-        y_early = keep.tile([P, 2, T], F32, name="y_early")
-        y_woven = [keep.tile([P, QCOLS, PACK], BF16, name="y_woven%d" % q, align_bytes=64) for q in range(QUARTERS)]
-        quarters = [slice(q * QCOLS, (q + 1) * QCOLS) for q in range(QUARTERS)]
+        y_early = keep.tile([P, 2 * T], F32, name="y_early")
+        y_woven = keep.tile([P, T * PACK], BF16, name="y_woven", align_bytes=64)
 
-        def weave_pair(u, q, source, copy):
+        def weave_pair(u, source, cols, copy):
             copy(
-                y_woven[q][:, :, 2 * u : 2 * u + 2].rearrange("p (c i) t -> p c t i", i=4),
-                source.rearrange("p t (c i) -> p c t i", i=4),
+                y_woven[:, cols.start * PACK : cols.stop * PACK].rearrange("p (c i u t) -> p u c t i", i=4, u=2, t=2)[:, u],
+                source[:].rearrange("p (t c) -> p t c", t=2)[:, :, cols].rearrange("p t (c i) -> p c t i", i=4),
             )
 
-        def halve(t):
-            halved = keep.tile([P, T], F32, name="halved", tag=("first2", "hi3")[t])
-            nc.scalar.activation(halved[:], res_planes[t][:], COPY, scale=0.5)
-            return halved
+        halved = keep.tile([P, 2 * T], F32, name="halved", tag="other3")
+        for t in range(2):
+            nc.scalar.activation(halved[:, t * T : (t + 1) * T], res_planes[t][:], COPY, scale=0.5)
 
-        windows[1] = keep.tile([P, T], F32, name="window1", tag="first3")
-        nc.gpsimd.memset(windows[1][:], 0.0)
-        scatter(0, 0, 2)
+        scatter(0, 0, 1)
+        scatter(0, 1, 2)
         scatter(1, 0, 2)
         for t in range(2):
             scatter(t, 2, GROUPS)
-            nc.gpsimd.tensor_tensor(y_early[:, t, :], windows[t][:], halve(t)[:], ALU.add)
-            nc.sync.dma_start(out_rows[t], y_early[:, t, :])
+            nc.gpsimd.tensor_tensor(y_early[:, t * T : (t + 1) * T], windows[t][:], halved[:, t * T : (t + 1) * T], ALU.add)
+            nc.sync.dma_start(out_rows[t], y_early[:, t * T : (t + 1) * T])
         scatter(2, 0, GROUPS)
-        y_late = keep.tile([P, 2 * T], F32, name="y_late", tag="mid3")
-        by_plane = y_late[:].rearrange("p (q t c) -> p t q c", q=QUARTERS, t=2)
-
-        def late(q, t):
-            return y_late[:, (2 * q + t) * QCOLS : (2 * q + t + 1) * QCOLS]
-
-        def quartered(plane):
-            return plane[:].rearrange("p (q c) -> p q c", q=QUARTERS)
-
-        nc.scalar.activation(by_plane[:, 1], quartered(res_planes[2]), COPY, scale=0.5)
-        for q in range(QUARTERS):
-            weave_pair(0, q, y_early[:, :, quarters[q]], nc.scalar.copy)
-        nc.gpsimd.tensor_tensor(by_plane[:, 0], quartered(windows[2]), by_plane[:, 1], ALU.add)
-        for q in range(QUARTERS):
-            nc.sync.dma_start(out_rows[2][:, quarters[q]], late(q, 0))
+        y_late = keep.tile([P, 2 * T], F32, name="y_late", tag="window0")
+        nc.scalar.activation(y_late[:, T:], res_planes[2][:], COPY, scale=0.5)
+        weave_pair(0, y_early, slice(0, T), nc.scalar.copy)
+        nc.gpsimd.tensor_tensor(y_late[:, :T], windows[2][:], y_late[:, T:], ALU.add)
+        nc.sync.dma_start(out_rows[2], y_late[:, :T])
         last = PACK - 1
+        shares = (slice(0, QCOLS), slice(QCOLS, VECTOR_FROM), slice(VECTOR_FROM, T))
         scatter(last, 0, GROUPS)
-        for q in range(QUARTERS):
+        for cols in shares:
             nc.vector.scalar_tensor_tensor(
-                late(q, 1), res_planes[last][:, quarters[q]], 0.5, windows[last][:, quarters[q]], ALU.mult, ALU.add
+                y_late[:, T + cols.start : T + cols.stop],
+                res_planes[last][:, cols],
+                0.5,
+                windows[last][:, cols],
+                ALU.mult,
+                ALU.add,
             )
-        nc.sync.dma_start(out_rows[last].rearrange("p (q c) -> p q c", q=QUARTERS), by_plane[:, 1])
-        for q in range(QUARTERS):
-            pair = y_late[:, 2 * q * QCOLS : 2 * (q + 1) * QCOLS].rearrange("p (t c) -> p t c", t=2)
-            weave_pair(1, q, pair, nc.scalar.copy if q < QUARTERS - 1 else nc.vector.tensor_copy)
+        nc.sync.dma_start(out_rows[last], y_late[:, T:])
+        for cols, copy in zip(shares, (nc.scalar.copy, nc.scalar.copy, nc.vector.tensor_copy)):
+            weave_pair(1, y_late, cols, copy)
 
         y_codes = keep.tile([P, T], U32, name="y_codes", align_bytes=64)
         y_scales = keep.tile([P, T], U8, name="y_scales", align_bytes=64)
         word_rows = out_1[0].rearrange("p c r -> p (c r)").bitcast(I32)
-        for q in (0, 3, 1, 2):
-            cols = slice(q * QCOLS, (q + 1) * QCOLS)
+        for cols in (slice(0, QCOLS), slice(T - QCOLS, T), slice(QCOLS, T - QCOLS)):
             nc.vector.quantize_mx(
                 out=y_codes[:, cols].bitcast(FP8X4),
                 scales=y_scales[:, cols],
-                in_=y_woven[q][:].rearrange("p c t -> p (c t)"),
+                in_=y_woven[:, cols.start * PACK : cols.stop * PACK],
             )
-            if q != 1:
-                ready = slice(QCOLS, 3 * QCOLS) if q == 2 else cols
-                nc.sync.dma_start(word_rows[:, ready], y_codes[:, ready].bitcast(I32))
+            nc.sync.dma_start(word_rows[:, cols], y_codes[:, cols].bitcast(I32))
         scale_rows = out_2[0].bitcast(I32)
         for quad in range(4):
             nc.scalar.dma_start(

from contextlib import ExitStack

import concourse.mybir as mybir
from concourse.masks import make_identity

K, T, J, N = 1024, 1024, 512, 512
FLOPS = 3 * 2 * K * N * J

F32 = mybir.dt.float32
BF16 = mybir.dt.bfloat16
I32 = mybir.dt.int32
U32 = mybir.dt.uint32
U16 = mybir.dt.uint16
U8 = mybir.dt.uint8
FP8X4 = mybir.dt.float8_e4m3fn_x4
FP4X4 = mybir.dt.float4_e2m1fn_x4
ALU = mybir.AluOpType
COPY = mybir.ActivationFunctionType.Copy
RELU = mybir.ActivationFunctionType.Relu

P = 128
PACK = 4
PASSES = K // (P * PACK)
GROUPS = J // P
LIST_COLS = P // 16
QCOLS = T // 4
VECTOR_FROM = 640


def tile_moe_middle_expert_of_three_pl_kernel(
    tc, xt, wa_words, wa_scales, wb_words, wb_scales, wc_words, wc_scales, ga, res, offs, out_0, out_1, out_2
):
    nc = tc.nc
    with ExitStack() as ctx:
        keep = ctx.enter_context(tc.tile_pool(name="keep", bufs=1))
        psum = ctx.enter_context(tc.psum_pool(name="psum", bufs=2))

        offsets = keep.tile([P, J // 16], U16, name="offsets")

        experts = (
            (wa_words, wa_scales, FP4X4, 2),
            (wb_words.rearrange("z p c r -> z p (c r)"), wb_scales, FP8X4, 4),
            (wc_words, wc_scales, FP4X4, 2),
        )
        w_scales = []
        for e in range(3):
            plane = keep.tile([P, PASSES * N], U8, name="w_scales%d" % e, align_bytes=64)
            nc.gpsimd.memset(plane[:].bitcast(I32), 0)
            w_scales.append(plane)

        x_rows = xt.rearrange("(z p t) c -> z t p c", z=PASSES, t=PACK)
        x_planes = {}
        w_words = {}

        def load_x(z, t):
            x_planes[z, t] = keep.tile([P, T], F32, name="x%d%d" % (z, t), align_bytes=64)
            nc.sync.dma_start(x_planes[z, t][:], x_rows[z, t])

        def load_words(e, passes):
            words, scales, dtype, width = experts[e]
            tile = keep.tile([P, len(passes) * width * N], U8, name="w_words%d%d" % (e, passes[0]), align_bytes=64)
            nc.sync.dma_start(
                tile[:].bitcast(I32).rearrange("p (z c) -> p z c", z=len(passes)),
                words[passes[0] : passes[-1] + 1].bitcast(I32).rearrange("z p c -> p z c"),
            )
            for n, z in enumerate(passes):
                w_words[e, z] = tile[:, n * width * N : (n + 1) * width * N]

        def load_scales(e, r, queue):
            rows = experts[e][1].bitcast(I32).rearrange("z (q r) c -> r q z c", r=4)
            queue.dma_start(w_scales[e][r:P:32, :].bitcast(I32).rearrange("q (z c) -> q z c", z=PASSES), rows[r])

        load_x(0, 0)
        nc.sync.dma_start(offsets[:], offs)
        load_x(0, 1)
        load_x(0, 2)
        load_x(0, 3)
        load_scales(0, 0, nc.sync)
        load_x(1, 0)
        load_scales(0, 1, nc.sync)
        load_words(1, [0])
        load_words(0, [0, 1])
        load_scales(0, 2, nc.sync)
        load_x(1, 1)
        load_scales(0, 3, nc.sync)
        load_x(1, 2)
        load_x(1, 3)
        load_words(1, [1])
        load_scales(2, 0, nc.sync)
        load_scales(2, 1, nc.sync)
        load_words(2, [0, 1])
        load_scales(2, 2, nc.sync)
        load_scales(2, 3, nc.sync)
        res_rows = res.rearrange("(p t) c -> t p c", t=PACK)
        res_planes = []
        for t in range(PACK):
            plane = keep.tile([P, T], F32, name="res%d" % t)
            nc.sync.dma_start(plane[:], res_rows[t])
            res_planes.append(plane)

        identity = keep.tile([P, P], F32, name="identity")
        make_identity(nc, identity[:])
        ga_rows = keep.tile([P, P], F32, name="ga_rows")
        nc.gpsimd.memset(ga_rows[:], 0.0)
        nc.gpsimd.dma_start(ga_rows[0:GROUPS, :], ga.rearrange("o (g p) -> (o g) p", p=P))
        for r in range(4):
            load_scales(1, r, nc.gpsimd)
        turned = psum.tile([P, PACK, P], F32, name="turned")
        nc.tensor.transpose(turned[:, 0, :], ga_rows[:], identity[:])
        gate = keep.tile([P, GROUPS], F32, name="gate")
        nc.scalar.activation(gate[:], turned[:, 0, 0:GROUPS], COPY)

        x_codes = {}
        x_scales = {}
        picked = [keep.tile([P, PACK * J], F32, name="picked%d" % z) for z in range(PASSES)]

        def gather(z, t, lo, hi):
            nc.vector.tensor_copy(
                picked[z][:, t * J + lo * P : t * J + hi * P],
                x_planes[z, t][:].indirect(offsets[:, lo * LIST_COLS : hi * LIST_COLS]),
            )

        def weave(z, g, count):
            woven = keep.tile([P, count * P, PACK], BF16, name="woven%d%d" % (z, g), align_bytes=64)
            nc.scalar.copy(
                woven[:].rearrange("p (c i) t -> p c t i", i=4),
                picked[z][:]
                .rearrange("p (t j) -> p t j", t=PACK)[:, :, g * P : (g + count) * P]
                .rearrange("p t (c i) -> p c t i", i=4),
            )
            return woven

        def quantise(z, g, count, woven, slot):
            codes = keep.tile([P, count * P], U32, name="x_codes", tag=slot, align_bytes=64)
            scales = keep.tile([P, count * P], U8, name="x_scales%d%d" % (z, g), align_bytes=64)
            nc.vector.quantize_mx(
                out=codes[:].bitcast(FP8X4),
                scales=scales[:],
                in_=woven[:].rearrange("p c t -> p (c t)"),
            )
            for n in range(count):
                x_codes[z, g + n] = codes[:, n * P : (n + 1) * P]
                x_scales[z, g + n] = scales[:, n * P : (n + 1) * P]

        sums = {}

        def multiply(e, z, g):
            if z == 0:
                sums[e, g] = psum.tile([P, N], F32, name="sum%d" % e)
            nc.tensor.matmul_mx(
                out=sums[e, g][:],
                lhsT=x_codes[z, g].bitcast(FP8X4),
                lhsT_scale=x_scales[z, g],
                rhs=w_words[e, z].bitcast(experts[e][2]),
                rhs_scale=w_scales[e][:, z * N : (z + 1) * N],
                start=(z == 0),
                stop=(z == PASSES - 1),
            )

        for t in range(PACK):
            gather(0, t, 0, GROUPS)
        first = [weave(0, 0, 1), weave(0, 1, 1), weave(0, 2, 2)]
        for t in range(PACK - 1):
            gather(1, t, 0, GROUPS)
            if t < 2:
                quantise(0, t, 1, first[t], "x1%d" % t)
                for e in range(2):
                    multiply(e, 0, t)
        gather(1, PACK - 1, 0, 1)
        gather(1, PACK - 1, 1, GROUPS)
        quantise(1, 0, 1, weave(1, 0, 1), "codes10")
        quantise(0, 2, 2, first[2], "x13")
        quantise(1, 1, 1, weave(1, 1, 1), "codes11")
        quantise(1, 2, 2, weave(1, 2, 2), "codes12")

        windows = {}
        for t, engine in ((0, nc.vector), (1, nc.vector), (2, nc.vector), (3, nc.gpsimd)):
            windows[t] = keep.tile([P, T], F32, name="window%d" % t)
            engine.memset(windows[t][:], 0.0)

        def dealt(bank):
            return bank[:].rearrange("p (m t) -> p t m", t=PACK)

        placed = keep.tile([P, PACK, J], F32, name="placed")

        def compare(g):
            for e in range(3):
                if g >= 2 or e == 2:
                    multiply(e, 0, g)
                multiply(e, 1, g)
            weight = gate[:, g : g + 1]
            first_answer = keep.tile([P, PACK, P], F32, name="first_answer%d" % g)
            if g == 0:
                nc.vector.tensor_scalar(first_answer[:], dealt(sums[0, g]), weight, None, ALU.mult)
            else:
                nc.scalar.activation(first_answer[:], dealt(sums[0, g]), COPY, scale=weight)
            hi = keep.tile([P, PACK, P], F32, name="hi%d" % g)
            nc.vector.scalar_tensor_tensor(hi[:], dealt(sums[1, g]), weight, first_answer[:], ALU.mult, ALU.max)
            lo = keep.tile([P, PACK, P], F32, name="lo%d" % g)
            nc.vector.scalar_tensor_tensor(lo[:], dealt(sums[1, g]), weight, first_answer[:], ALU.mult, ALU.min)
            capped = keep.tile([P, PACK, P], F32, name="capped%d" % g)
            nc.vector.scalar_tensor_tensor(capped[:], dealt(sums[2, g]), weight, hi[:], ALU.mult, ALU.min)
            other = keep.tile([P, PACK, P], F32, name="other", tag="other%d" % g)
            if g < GROUPS - 1:
                nc.gpsimd.tensor_tensor(other[:], lo[:], capped[:], ALU.subtract)
            else:
                nc.vector.tensor_tensor(other[:], lo[:], capped[:], ALU.max)
            return capped, other

        def place(g, capped, other):
            if g < GROUPS - 1:
                lift = keep.tile([P, PACK, P], F32, name="lift%d" % g)
                nc.scalar.activation(lift[:], other[:], RELU)
                parts = (capped, lift)
            else:
                parts = (other,)
            turned = psum.tile([P, PACK, P], F32, name="turned")
            for t in range(PACK):
                for n, source in enumerate(parts):
                    nc.tensor.matmul(
                        turned[:, t, :],
                        source[:, t, :],
                        identity[:],
                        start=n == 0,
                        stop=n == len(parts) - 1,
                        is_transpose=True,
                    )
            nc.scalar.copy(placed[:, :, g * P : (g + 1) * P], turned[:])

        compared = [compare(g) for g in range(GROUPS)]
        for g in range(GROUPS):
            place(g, *compared[g])

        def scatter(t, lo, hi):
            nc.vector.tensor_copy(
                windows[t][:].indirect(offsets[:, lo * LIST_COLS : hi * LIST_COLS]),
                placed[:, t, lo * P : hi * P],
            )

        out_rows = out_0.rearrange("(p t) c -> t p c", t=PACK)
        y_early = keep.tile([P, 2 * T], F32, name="y_early")
        y_woven = keep.tile([P, T * PACK], BF16, name="y_woven", align_bytes=64)

        def weave_pair(u, source, cols, copy):
            copy(
                y_woven[:, cols.start * PACK : cols.stop * PACK].rearrange("p (c i u t) -> p u c t i", i=4, u=2, t=2)[:, u],
                source[:].rearrange("p (t c) -> p t c", t=2)[:, :, cols].rearrange("p t (c i) -> p c t i", i=4),
            )

        halved = keep.tile([P, 2 * T], F32, name="halved", tag="other3")
        for t in range(2):
            nc.scalar.activation(halved[:, t * T : (t + 1) * T], res_planes[t][:], COPY, scale=0.5)

        scatter(0, 0, 1)
        scatter(0, 1, 2)
        scatter(1, 0, 2)
        for t in range(2):
            scatter(t, 2, GROUPS)
            nc.gpsimd.tensor_tensor(y_early[:, t * T : (t + 1) * T], windows[t][:], halved[:, t * T : (t + 1) * T], ALU.add)
            nc.sync.dma_start(out_rows[t], y_early[:, t * T : (t + 1) * T])
        scatter(2, 0, GROUPS)
        y_late = keep.tile([P, 2 * T], F32, name="y_late", tag="window0")
        nc.scalar.activation(y_late[:, T:], res_planes[2][:], COPY, scale=0.5)
        weave_pair(0, y_early, slice(0, T), nc.scalar.copy)
        nc.gpsimd.tensor_tensor(y_late[:, :T], windows[2][:], y_late[:, T:], ALU.add)
        nc.sync.dma_start(out_rows[2], y_late[:, :T])
        last = PACK - 1
        shares = (slice(0, QCOLS), slice(QCOLS, VECTOR_FROM), slice(VECTOR_FROM, T))
        scatter(last, 0, GROUPS)
        for cols in shares:
            nc.vector.scalar_tensor_tensor(
                y_late[:, T + cols.start : T + cols.stop],
                res_planes[last][:, cols],
                0.5,
                windows[last][:, cols],
                ALU.mult,
                ALU.add,
            )
        nc.sync.dma_start(out_rows[last], y_late[:, T:])
        for cols, copy in zip(shares, (nc.scalar.copy, nc.scalar.copy, nc.vector.tensor_copy)):
            weave_pair(1, y_late, cols, copy)

        y_codes = keep.tile([P, T], U32, name="y_codes", align_bytes=64)
        y_scales = keep.tile([P, T], U8, name="y_scales", align_bytes=64)
        word_rows = out_1[0].rearrange("p c r -> p (c r)").bitcast(I32)
        for cols in (slice(0, QCOLS), slice(T - QCOLS, T), slice(QCOLS, T - QCOLS)):
            nc.vector.quantize_mx(
                out=y_codes[:, cols].bitcast(FP8X4),
                scales=y_scales[:, cols],
                in_=y_woven[:, cols.start * PACK : cols.stop * PACK],
            )
            nc.sync.dma_start(word_rows[:, cols], y_codes[:, cols].bitcast(I32))
        scale_rows = out_2[0].bitcast(I32)
        for quad in range(4):
            nc.scalar.dma_start(
                scale_rows[4 * quad : 4 * quad + 4, :], y_scales[32 * quad : 32 * quad + 4, :].bitcast(I32)
            )
